import numpy as np
import ml_dtypes


def mxq(x, axis, fmt="e4m3"):
    dtype, down = {"e4m3": (ml_dtypes.float8_e4m3fn, 7), "e5m2": (ml_dtypes.float8_e5m2, 14)}[fmt]
    v = np.moveaxis(np.asarray(x, np.float32).astype(ml_dtypes.bfloat16).astype(np.float64), axis, -1)
    blocks = v.reshape(v.shape[:-1] + (-1, 32))
    amax = np.abs(blocks).max(-1, keepdims=True)
    byte = np.maximum(np.where(amax > 0, np.frexp(amax)[1] - 1 + 127, 0) - down, 1)
    scale = np.exp2(byte - 127.0)
    codes = (blocks / scale).astype(np.float32).astype(dtype).astype(np.float64)
    return np.moveaxis((codes * scale).reshape(v.shape), -1, axis)


WIDE = False


def mx_kscale(k):
    if not WIDE:
        return np.ones(k)
    levels = np.array([30, -30])
    if k % 512:
        return np.exp2(np.random.permutation(np.resize(levels, k // 32))).repeat(32)
    a = np.empty((k // 512, 16))
    for p in range(k // 512):
        a[p, :8] = np.random.permutation(np.resize(levels, 8))
        for g in range(8):
            far = levels[np.abs(levels - a[p, g]) >= 10]
            a[p, g + 8] = far[np.random.randint(len(far))]
    return np.exp2(a.ravel()).repeat(32)


def f64(x):
    return np.asarray(x).astype(np.float64)


def striped(idx):
    return np.tile(np.asarray(idx).reshape(-1, 16).T, (8, 1)).astype(np.uint16)


def unstriped(offs):
    return offs[:16].T.reshape(-1).astype(np.int64)


E2M1 = np.array([0.0, 0.5, 1.0, 1.5, 2.0, 3.0, 4.0, 6.0, -0.0, -0.5, -1.0, -1.5, -2.0, -3.0, -4.0, -6.0])


def pack_weight(w, fmt):
    k, n = w.shape
    w = f64(np.asarray(w, np.float32).astype(ml_dtypes.bfloat16)).reshape(k // 32, 32, n)
    amax = np.abs(w).max(1)
    if fmt == "e4m3":
        byte = np.frexp(amax)[1] - 1 + 127 - 7
    else:
        mant, ex = np.frexp(amax / 6.0)
        byte = np.where(mant > 0.5, ex, ex - 1) + 127
    byte = np.clip(np.where(amax > 0, byte, 1), 1, 254)
    scaled = (w * np.exp2(127.0 - byte)[:, None, :]).reshape(k, n).astype(np.float32)
    by_word = np.ascontiguousarray(scaled.reshape(k // 512, 128, 4, n).transpose(0, 1, 3, 2))
    if fmt == "e4m3":
        words = by_word.astype(ml_dtypes.float8_e4m3fn).view(np.uint8)
    else:
        c = by_word.astype(ml_dtypes.float4_e2m1fn).view(np.uint8) & 0xF
        words = (c[..., 0::2] | (c[..., 1::2] << 4)).reshape(k // 512, 128, 2 * n)
    return np.ascontiguousarray(words), np.ascontiguousarray(byte.astype(np.uint8).reshape(k // 512, 16, n))


def unpack_weight(words, scales, fmt):
    g, _, n = scales.shape
    words = np.ascontiguousarray(words).reshape(g, 128, n, -1)
    if fmt == "e4m3":
        vals = words.view(ml_dtypes.float8_e4m3fn).astype(np.float64)
    else:
        nib = np.empty((g, 128, n, 4), np.uint8)
        nib[..., 0::2] = words & 0xF
        nib[..., 1::2] = words >> 4
        vals = E2M1[nib]
    vals = vals * np.repeat(np.exp2(scales.astype(np.float64) - 127.0), 8, axis=1)[..., None]
    return vals.transpose(0, 1, 3, 2).reshape(g * 512, n)


K, T, J, R, O, N, L, E = 512, 2048, 256, 512, 128, 256, 512, 1024


def setup_inputs():
    n = np.random.standard_normal
    idx = np.random.permutation(T)[:J]
    idx2 = np.random.permutation(T)[:J]
    idx3 = np.random.permutation(T)[:J]
    idx4 = np.random.permutation(J)[:O]
    idx5 = np.random.permutation(J)[:O]
    idx6 = np.random.permutation(E)[:O]
    fk = mx_kscale(K)
    fr = mx_kscale(R)
    fl = mx_kscale(L)
    xtp = pack_weight(n((K, T)) / fk[:, None], "e2m1")
    wp = pack_weight(n((K, R)) * 1 / np.sqrt(K) * fk[:, None] * fr, "e4m3")
    wbp = pack_weight(n((R, N)) * 1 / np.sqrt(R) / fr[:, None], "e2m1")
    sxp = pack_weight(n((L, O)) / fl[:, None], "e4m3")
    wsp = pack_weight(n((L, N)) * 1 / np.sqrt(L) * fl[:, None], "e4m3")
    return {
        "xt_words": xtp[0],
        "xt_scales": xtp[1],
        "w_words": wp[0],
        "w_scales": wp[1],
        "wb_words": wbp[0],
        "wb_scales": wbp[1],
        "sx_words": sxp[0],
        "sx_scales": sxp[1],
        "ws_words": wsp[0],
        "ws_scales": wsp[1],
        "offs": striped(idx),
        "offs2": striped(idx2),
        "offs3": striped(idx3),
        "offs4": striped(idx4),
        "offs5": striped(idx5),
        "offs6": striped(idx6),
    }


def reference(xt_words, xt_scales, w_words, w_scales, wb_words, wb_scales, sx_words, sx_scales, ws_words, ws_scales, offs, offs2, offs3, offs4, offs5, offs6):
    idx = unstriped(offs)
    idx2 = unstriped(offs2)
    idx3 = unstriped(offs3)
    idx4 = unstriped(offs4)
    idx5 = unstriped(offs5)
    idx6 = unstriped(offs6)
    xtu = unpack_weight(xt_words, xt_scales, "e2m1")
    wu = unpack_weight(w_words, w_scales, "e4m3")
    wbu = unpack_weight(wb_words, wb_scales, "e2m1")
    sxu = unpack_weight(sx_words, sx_scales, "e4m3")
    wsu = unpack_weight(ws_words, ws_scales, "e4m3")
    xtidxg = xtu[:, idx]
    a = wu.T @ xtidxg
    xtidx2g = xtu[:, idx2]
    b = wu.T @ xtidx2g
    xtidx3g = xtu[:, idx3]
    g0 = wu.T @ xtidx3g
    c1 = np.maximum(b, g0)
    hid = np.abs(a[:, idx4] - c1[:, idx5])
    hidq = mxq(hid, 0, "e5m2")
    p = wbu.T @ hidq + wsu.T @ sxu
    y = np.zeros((N, E))
    y[:, idx6] = p
    return y

@@ -1,0 +1,165 @@
+from contextlib import ExitStack
+
+import concourse.mybir as mybir
+
+K, T, J, R, O, N, L, E = 512, 2048, 256, 512, 128, 256, 512, 1024
+FLOPS = 2 * (3 * K * R * J + R * N * O + L * N * O)
+
+F32 = mybir.dt.float32
+BF16 = mybir.dt.bfloat16
+I32 = mybir.dt.int32
+U32 = mybir.dt.uint32
+U16 = mybir.dt.uint16
+U8 = mybir.dt.uint8
+E4M3X4 = mybir.dt.float8_e4m3fn_x4
+E5M2X4 = mybir.dt.float8_e5m2_x4
+E2M1X4 = mybir.dt.float4_e2m1fn_x4
+ALU = mybir.AluOpType
+ACT = mybir.ActivationFunctionType
+
+P = 128
+PACK = 4
+O_SCALAR = 64
+
+
+def load_scale_rows(queue, plane, scales):
+    for q in range(4):
+        queue.dma_start(plane[32 * q : 32 * q + 4, :].bitcast(I32), scales[0, 4 * q : 4 * q + 4, :].bitcast(I32))
+
+
+def tile_list_triple_looked_skip_scattered_kernel(
+    tc, xt_words, xt_scales, w_words, w_scales, wb_words, wb_scales, sx_words, sx_scales, ws_words, ws_scales,
+    offs, offs2, offs3, offs4, offs5, offs6, out,
+):
+    nc = tc.nc
+    with ExitStack() as ctx:
+        lists = ctx.enter_context(tc.tile_pool(name="lists", bufs=1))
+        sb = ctx.enter_context(tc.tile_pool(name="sb", bufs=1))
+        psum = ctx.enter_context(tc.psum_pool(name="psum", bufs=1))
+
+        def load_list(src, name):
+            tile = lists.tile(list(src.shape), U16, name=name)
+            nc.sync.dma_start(tile[:], src)
+            return tile
+
+        xt_w = sb.tile([P, T], U16, name="xt_w", align_bytes=64)
+        xt_s = sb.tile([P, T], U8, name="xt_s", align_bytes=64)
+        w_raw = sb.tile([P, R], U32, name="w_raw", align_bytes=64)
+        w_raw_s = sb.tile([P, R], U8, name="w_raw_s", align_bytes=64)
+        w_w = sb.tile([P, R], U32, name="w_w", align_bytes=64)
+        w_s = sb.tile([P, R], U8, name="w_s", align_bytes=64)
+        wb_w = sb.tile([P, 2 * N], U8, name="wb_w", align_bytes=64)
+        ws_w = sb.tile([P, N], U32, name="ws_w", align_bytes=64)
+        sx_w = sb.tile([P, O], U32, name="sx_w", align_bytes=64)
+        late_s = sb.tile([P, N + N + O], U8, name="late_s", align_bytes=64)
+        wb_s, ws_s, sx_s = late_s[:, 0:N], late_s[:, N : 2 * N], late_s[:, 2 * N : 2 * N + O]
+        pages = [sb.tile([P, E], F32, name=f"page{h}") for h in range(2)]
+
+        nc.gpsimd.memset(xt_s[:].bitcast(I32), 0)
+        nc.vector.memset(w_raw_s[:].bitcast(I32), 0)
+        nc.vector.memset(late_s[:].bitcast(I32), 0)
+
+        nc.sync.dma_start(xt_w[:].bitcast(I32), xt_words[0].bitcast(I32))
+        load_scale_rows(nc.sync, xt_s, xt_scales)
+        list_a = load_list(offs, "list_a")
+        list_b = load_list(offs2, "list_b")
+        nc.sync.dma_start(w_raw[:].bitcast(I32), w_words[0].rearrange("p n t -> p (n t)").bitcast(I32))
+        load_scale_rows(nc.sync, w_raw_s, w_scales)
+        list_g = load_list(offs3, "list_g")
+        pick_a = load_list(offs4, "pick_a")
+        pick_c = load_list(offs5, "pick_c")
+        nc.gpsimd.dma_start(ws_w[:].bitcast(I32), ws_words[0].rearrange("p n t -> p (n t)").bitcast(I32))
+        nc.gpsimd.dma_start(sx_w[:].bitcast(I32), sx_words[0].rearrange("p n t -> p (n t)").bitcast(I32))
+        nc.gpsimd.dma_start(wb_w[:].bitcast(I32), wb_words[0].bitcast(I32))
+        load_scale_rows(nc.sync, ws_s, ws_scales)
+        load_scale_rows(nc.sync, sx_s, sx_scales)
+        load_scale_rows(nc.sync, wb_s, wb_scales)
+        places = load_list(offs6, "places")
+
+        for page in pages:
+            nc.vector.memset(page[:], 0.0)
+
+        nc.gpsimd.tensor_copy(
+            w_w[:].rearrange("p (t c i) -> p c t i", t=PACK, i=4),
+            w_raw[:].rearrange("p (c i t) -> p c t i", t=PACK, i=4),
+        )
+        for h in range(2):
+            nc.gpsimd.tensor_copy(
+                w_s[:].rearrange("p (t c i) -> p c t i", t=PACK, i=16)[:, :, 2 * h : 2 * h + 2, :],
+                w_raw_s[:].rearrange("p (c i t) -> p c t i", t=PACK, i=16)[:, :, 2 * h : 2 * h + 2, :],
+            )
+
+        def gather_tokens(token_list, name):
+            words = sb.tile([P, J], U16, name=name + "_w", align_bytes=64)
+            scales = sb.tile([P, J], U8, name=name + "_s", align_bytes=64)
+            nc.vector.tensor_copy(words[:], xt_w[:].indirect(token_list[:]))
+            nc.vector.tensor_copy(scales[:], xt_s[:].indirect(token_list[:]))
+            return words, scales
+
+        def first_matrix(dst, t, tokens):
+            words, scales = tokens
+            cols = slice(t * P, (t + 1) * P)
+            nc.tensor.matmul_mx(
+                out=dst, lhsT=w_w[:, cols].bitcast(E4M3X4), lhsT_scale=w_s[:, cols],
+                rhs=words[:].bitcast(E2M1X4), rhs_scale=scales[:], start=True, stop=True,
+            )
+
+        tokens_a = gather_tokens(list_a, "tok_a")
+        tokens_b = gather_tokens(list_b, "tok_b")
+        tokens_g = gather_tokens(list_g, "tok_g")
+
+        def through_sbuf(tokens, name, first_bank):
+            halves = []
+            for h in range(2):
+                acc = psum.tile([P, 2, J], F32, name=f"{name}_ps{h}", tag=f"bank{first_bank + h}")
+                for i in range(2):
+                    first_matrix(acc[:, i, :], 2 * h + i, tokens)
+                held = sb.tile([P, 2, J], F32, name=f"{name}_sb{h}")
+                nc.scalar.activation(held[:], acc[:], ACT.Copy)
+                halves.append(held)
+            return [halves[t // 2][:, t % 2, :] for t in range(PACK)]
+
+        a_sb = through_sbuf(tokens_a, "a", 0)
+        b_sb = through_sbuf(tokens_b, "b", 2)
+
+        a_picked = sb.tile([P, PACK, O], F32, name="a_picked")
+        diff = sb.tile([P, PACK, O], F32, name="diff")
+        for t in range(PACK):
+            g_ps = psum.tile([P, J], F32, name=f"g_ps{t}", tag=f"bank{4 + t}")
+            first_matrix(g_ps[:], t, tokens_g)
+            nc.scalar.activation(a_picked[:, t, :], a_sb[t].indirect(pick_a[:]), ACT.Copy)
+            c1 = sb.tile([P, J], F32, name=f"c1_{t}")
+            nc.vector.tensor_tensor(c1[:], g_ps[:], b_sb[t], ALU.max)
+            nc.vector.tensor_tensor(diff[:, t, :], c1[:].indirect(pick_c[:]), a_picked[:, t, :], ALU.subtract)
+
+        p_ps = [psum.tile([P, O], F32, name=f"p_ps{h}", tag=f"bank{h}") for h in range(2)]
+        for h in range(2):
+            cols = slice(h * P, (h + 1) * P)
+            nc.tensor.matmul_mx(
+                out=p_ps[h][:], lhsT=ws_w[:, cols].bitcast(E4M3X4), lhsT_scale=ws_s[:, cols],
+                rhs=sx_w[:].bitcast(E4M3X4), rhs_scale=sx_s, start=True, stop=False,
+            )
+
+        hid = sb.tile([P, O, PACK], BF16, name="hid", align_bytes=64)
+        by_place = diff[:].rearrange("p t o -> p o t")
+        nc.scalar.activation(hid[:, :O_SCALAR, :], by_place[:, :O_SCALAR, :], ACT.Abs)
+        nc.vector.scalar_tensor_tensor(
+            hid[:, O_SCALAR:, :], by_place[:, O_SCALAR:, :], -1.0, by_place[:, O_SCALAR:, :], ALU.mult, ALU.max
+        )
+        hid_w = sb.tile([P, O], U32, name="hid_w", align_bytes=64)
+        hid_s = sb.tile([P, O], U8, name="hid_s", align_bytes=64)
+        nc.vector.quantize_mx(out=hid_w[:].bitcast(E5M2X4), scales=hid_s[:], in_=hid[:].rearrange("p o t -> p (o t)"))
+
+        for h in range(2):
+            nc.tensor.matmul_mx(
+                out=p_ps[h][:], lhsT=wb_w[:, 2 * h * P : 2 * (h + 1) * P].bitcast(E2M1X4),
+                lhsT_scale=wb_s[:, h * P : (h + 1) * P],
+                rhs=hid_w[:].bitcast(E5M2X4), rhs_scale=hid_s[:], start=False, stop=True,
+            )
+        p_sb = [sb.tile([P, O], F32, name=f"p_sb{h}") for h in range(2)]
+        nc.vector.tensor_copy(p_sb[0][:], p_ps[0][:])
+        nc.vector.tensor_copy(pages[0][:].indirect(places[:]), p_sb[0][:])
+        nc.sync.dma_start(out[0:P, :], pages[0][:])
+        nc.scalar.copy(p_sb[1][:], p_ps[1][:])
+        nc.scalar.activation(pages[1][:].indirect(places[:]), p_sb[1][:], ACT.Copy)
+        nc.scalar.dma_start(out[P : 2 * P, :], pages[1][:])

@@ -55,22 +55,22 @@ def tile_list_triple_looked_skip_scattered_kernel(
         wb_s, ws_s, sx_s = late_s[:, 0:N], late_s[:, N : 2 * N], late_s[:, 2 * N : 2 * N + O]
         pages = [sb.tile([P, E], F32, name=f"page{h}") for h in range(2)]
 
-        nc.gpsimd.memset(xt_s[:].bitcast(I32), 0)
-        nc.vector.memset(w_raw_s[:].bitcast(I32), 0)
-        nc.vector.memset(late_s[:].bitcast(I32), 0)
+        nc.vector.memset(xt_s[:].bitcast(I32), 0)
+        nc.gpsimd.memset(w_raw_s[:].bitcast(I32), 0)
+        nc.gpsimd.memset(late_s[:].bitcast(I32), 0)
 
         nc.sync.dma_start(xt_w[:].bitcast(I32), xt_words[0].bitcast(I32))
-        load_scale_rows(nc.sync, xt_s, xt_scales)
         list_a = load_list(offs, "list_a")
         list_b = load_list(offs2, "list_b")
+        load_scale_rows(nc.sync, xt_s, xt_scales)
         nc.sync.dma_start(w_raw[:].bitcast(I32), w_words[0].rearrange("p n t -> p (n t)").bitcast(I32))
-        load_scale_rows(nc.sync, w_raw_s, w_scales)
         list_g = load_list(offs3, "list_g")
+        load_scale_rows(nc.sync, w_raw_s, w_scales)
         pick_a = load_list(offs4, "pick_a")
         pick_c = load_list(offs5, "pick_c")
-        nc.gpsimd.dma_start(ws_w[:].bitcast(I32), ws_words[0].rearrange("p n t -> p (n t)").bitcast(I32))
-        nc.gpsimd.dma_start(sx_w[:].bitcast(I32), sx_words[0].rearrange("p n t -> p (n t)").bitcast(I32))
-        nc.gpsimd.dma_start(wb_w[:].bitcast(I32), wb_words[0].bitcast(I32))
+        nc.sync.dma_start(ws_w[:].bitcast(I32), ws_words[0].rearrange("p n t -> p (n t)").bitcast(I32))
+        nc.sync.dma_start(sx_w[:].bitcast(I32), sx_words[0].rearrange("p n t -> p (n t)").bitcast(I32))
+        nc.sync.dma_start(wb_w[:].bitcast(I32), wb_words[0].bitcast(I32))
         load_scale_rows(nc.sync, ws_s, ws_scales)
         load_scale_rows(nc.sync, sx_s, sx_scales)
         load_scale_rows(nc.sync, wb_s, wb_scales)
@@ -79,15 +79,12 @@ def tile_list_triple_looked_skip_scattered_kernel(
         for page in pages:
             nc.vector.memset(page[:], 0.0)
 
-        nc.gpsimd.tensor_copy(
+        nc.scalar.copy(
             w_w[:].rearrange("p (t c i) -> p c t i", t=PACK, i=4),
             w_raw[:].rearrange("p (c i t) -> p c t i", t=PACK, i=4),
         )
-        for h in range(2):
-            nc.gpsimd.tensor_copy(
-                w_s[:].rearrange("p (t c i) -> p c t i", t=PACK, i=16)[:, :, 2 * h : 2 * h + 2, :],
-                w_raw_s[:].rearrange("p (c i t) -> p c t i", t=PACK, i=16)[:, :, 2 * h : 2 * h + 2, :],
-            )
+        for t in range(PACK):
+            nc.gpsimd.tensor_copy(w_s[:, t * P : (t + 1) * P], w_raw_s[:, t::PACK])
 
         def gather_tokens(token_list, name):
             words = sb.tile([P, J], U16, name=name + "_w", align_bytes=64)
@@ -108,31 +105,48 @@ def tile_list_triple_looked_skip_scattered_kernel(
         tokens_b = gather_tokens(list_b, "tok_b")
         tokens_g = gather_tokens(list_g, "tok_g")
 
-        def through_sbuf(tokens, name, first_bank):
-            halves = []
-            for h in range(2):
-                acc = psum.tile([P, 2, J], F32, name=f"{name}_ps{h}", tag=f"bank{first_bank + h}")
-                for i in range(2):
-                    first_matrix(acc[:, i, :], 2 * h + i, tokens)
-                held = sb.tile([P, 2, J], F32, name=f"{name}_sb{h}")
-                nc.scalar.activation(held[:], acc[:], ACT.Copy)
-                halves.append(held)
-            return [halves[t // 2][:, t % 2, :] for t in range(PACK)]
-
-        a_sb = through_sbuf(tokens_a, "a", 0)
-        b_sb = through_sbuf(tokens_b, "b", 2)
-
         a_picked = sb.tile([P, PACK, O], F32, name="a_picked")
         diff = sb.tile([P, PACK, O], F32, name="diff")
-        for t in range(PACK):
-            g_ps = psum.tile([P, J], F32, name=f"g_ps{t}", tag=f"bank{4 + t}")
-            first_matrix(g_ps[:], t, tokens_g)
-            nc.scalar.activation(a_picked[:, t, :], a_sb[t].indirect(pick_a[:]), ACT.Copy)
-            c1 = sb.tile([P, J], F32, name=f"c1_{t}")
-            nc.vector.tensor_tensor(c1[:], g_ps[:], b_sb[t], ALU.max)
-            nc.vector.tensor_tensor(diff[:, t, :], c1[:].indirect(pick_c[:]), a_picked[:, t, :], ALU.subtract)
+        c1 = [sb.tile([P, J], F32, name=f"c1_{t}") for t in range(PACK)]
 
-        p_ps = [psum.tile([P, O], F32, name=f"p_ps{h}", tag=f"bank{h}") for h in range(2)]
+        def product(tokens, slots, name, bank):
+            acc = psum.tile([P, len(slots), J], F32, name=name, tag=f"bank{bank}")
+            for i, t in enumerate(slots):
+                first_matrix(acc[:, i, :], t, tokens)
+            return acc
+
+        def to_sbuf(acc, name, tag):
+            held = sb.tile(list(acc.shape), F32, name=name, tag=tag, align_bytes=64)
+            nc.scalar.copy(held[:], acc[:])
+            return held
+
+        def pick_from_a(a_sb, slots):
+            for i, t in enumerate(slots):
+                nc.scalar.activation(a_picked[:, t, :], a_sb[:, i, :].indirect(pick_a[:]), ACT.Copy)
+
+        def subtract(t):
+            nc.vector.tensor_tensor(diff[:, t, :], c1[t][:].indirect(pick_c[:]), a_picked[:, t, :], ALU.subtract)
+
+        pick_from_a(to_sbuf(product(tokens_a, [0], "a0", 0), "a0_sb", "a0_sb"), [0])
+        bg0 = psum.tile([P, 2, J], F32, name="bg0", tag="bank2")
+        first_matrix(bg0[:, 0, :], 0, tokens_b)
+        pick_from_a(to_sbuf(product(tokens_a, [1], "a1", 1), "a1_sb", "a1_sb"), [1])
+        first_matrix(bg0[:, 1, :], 0, tokens_g)
+        nc.vector.tensor_reduce(c1[0][:], bg0[:].rearrange("p s j -> p j s"), mybir.AxisListType.X, ALU.max)
+        subtract(0)
+        b1_sb = to_sbuf(product(tokens_b, [1], "b1", 3), "b1_sb", "b1_sb")
+        g1 = product(tokens_g, [1], "g1", 4)
+        nc.vector.tensor_tensor(c1[1][:], g1[:, 0, :], b1_sb[:, 0, :], ALU.max)
+        subtract(1)
+        b23_sb = to_sbuf(product(tokens_b, [2, 3], "b23", 5), "b23_sb", "b23_sb")
+        pick_from_a(to_sbuf(product(tokens_a, [2, 3], "a23", 6), "a23_sb", "a23_then_hid"), [2, 3])
+        for t, bank in ((2, 7), (3, 0)):
+            g_t = product(tokens_g, [t], f"g{t}", bank)
+            nc.vector.tensor_tensor(c1[t][:], g_t[:, 0, :], b23_sb[:, t - 2, :], ALU.max)
+        subtract(2)
+        subtract(3)
+
+        p_ps = [psum.tile([P, O], F32, name=f"p_ps{h}", tag=f"bank{1 + 2 * h}") for h in range(2)]
         for h in range(2):
             cols = slice(h * P, (h + 1) * P)
             nc.tensor.matmul_mx(
@@ -140,12 +154,12 @@ def tile_list_triple_looked_skip_scattered_kernel(
                 rhs=sx_w[:].bitcast(E4M3X4), rhs_scale=sx_s, start=True, stop=False,
             )
 
-        hid = sb.tile([P, O, PACK], BF16, name="hid", align_bytes=64)
+        hid = sb.tile([P, O, PACK], BF16, name="hid", tag="a23_then_hid", align_bytes=64)
         by_place = diff[:].rearrange("p t o -> p o t")
-        nc.scalar.activation(hid[:, :O_SCALAR, :], by_place[:, :O_SCALAR, :], ACT.Abs)
-        nc.vector.scalar_tensor_tensor(
-            hid[:, O_SCALAR:, :], by_place[:, O_SCALAR:, :], -1.0, by_place[:, O_SCALAR:, :], ALU.mult, ALU.max
-        )
+        nc.scalar.activation(hid[:, :, 0:2], by_place[:, :, 0:2], ACT.Abs)
+        nc.scalar.activation(hid[:, :O_SCALAR, 2:4], by_place[:, :O_SCALAR, 2:4], ACT.Abs)
+        late = by_place[:, O_SCALAR:, 2:4]
+        nc.vector.scalar_tensor_tensor(hid[:, O_SCALAR:, 2:4], late, -1.0, late, ALU.mult, ALU.max)
         hid_w = sb.tile([P, O], U32, name="hid_w", align_bytes=64)
         hid_s = sb.tile([P, O], U8, name="hid_s", align_bytes=64)
         nc.vector.quantize_mx(out=hid_w[:].bitcast(E5M2X4), scales=hid_s[:], in_=hid[:].rearrange("p o t -> p (o t)"))

@@ -64,8 +64,8 @@ def tile_list_triple_looked_skip_scattered_kernel(
         list_b = load_list(offs2, "list_b")
         load_scale_rows(nc.sync, xt_s, xt_scales)
         nc.sync.dma_start(w_raw[:].bitcast(I32), w_words[0].rearrange("p n t -> p (n t)").bitcast(I32))
-        list_g = load_list(offs3, "list_g")
         load_scale_rows(nc.sync, w_raw_s, w_scales)
+        list_g = load_list(offs3, "list_g")
         pick_a = load_list(offs4, "pick_a")
         pick_c = load_list(offs5, "pick_c")
         nc.sync.dma_start(ws_w[:].bitcast(I32), ws_words[0].rearrange("p n t -> p (n t)").bitcast(I32))
@@ -83,8 +83,6 @@ def tile_list_triple_looked_skip_scattered_kernel(
             w_w[:].rearrange("p (t c i) -> p c t i", t=PACK, i=4),
             w_raw[:].rearrange("p (c i t) -> p c t i", t=PACK, i=4),
         )
-        for t in range(PACK):
-            nc.gpsimd.tensor_copy(w_s[:, t * P : (t + 1) * P], w_raw_s[:, t::PACK])
 
         def gather_tokens(token_list, name):
             words = sb.tile([P, J], U16, name=name + "_w", align_bytes=64)
@@ -103,6 +101,10 @@ def tile_list_triple_looked_skip_scattered_kernel(
 
         tokens_a = gather_tokens(list_a, "tok_a")
         tokens_b = gather_tokens(list_b, "tok_b")
+        nc.vector.tensor_copy(
+            w_s[:].rearrange("p (t c i) -> p c t i", t=PACK, i=16),
+            w_raw_s[:].rearrange("p (c i t) -> p c t i", t=PACK, i=16),
+        )
         tokens_g = gather_tokens(list_g, "tok_g")
 
         a_picked = sb.tile([P, PACK, O], F32, name="a_picked")
@@ -131,10 +133,10 @@ def tile_list_triple_looked_skip_scattered_kernel(
         bg0 = psum.tile([P, 2, J], F32, name="bg0", tag="bank2")
         first_matrix(bg0[:, 0, :], 0, tokens_b)
         pick_from_a(to_sbuf(product(tokens_a, [1], "a1", 1), "a1_sb", "a1_sb"), [1])
+        b1_sb = to_sbuf(product(tokens_b, [1], "b1", 3), "b1_sb", "b1_sb")
         first_matrix(bg0[:, 1, :], 0, tokens_g)
         nc.vector.tensor_reduce(c1[0][:], bg0[:].rearrange("p s j -> p j s"), mybir.AxisListType.X, ALU.max)
         subtract(0)
-        b1_sb = to_sbuf(product(tokens_b, [1], "b1", 3), "b1_sb", "b1_sb")
         g1 = product(tokens_g, [1], "g1", 4)
         nc.vector.tensor_tensor(c1[1][:], g1[:, 0, :], b1_sb[:, 0, :], ALU.max)
         subtract(1)

from contextlib import ExitStack

import concourse.mybir as mybir

K, T, J, R, O, N, L, E = 512, 2048, 256, 512, 128, 256, 512, 1024
FLOPS = 2 * (3 * K * R * J + R * N * O + L * N * O)

F32 = mybir.dt.float32
BF16 = mybir.dt.bfloat16
I32 = mybir.dt.int32
U32 = mybir.dt.uint32
U16 = mybir.dt.uint16
U8 = mybir.dt.uint8
E4M3X4 = mybir.dt.float8_e4m3fn_x4
E5M2X4 = mybir.dt.float8_e5m2_x4
E2M1X4 = mybir.dt.float4_e2m1fn_x4
ALU = mybir.AluOpType
ACT = mybir.ActivationFunctionType

P = 128
PACK = 4
O_SCALAR = 64


def load_scale_rows(queue, plane, scales):
    for q in range(4):
        queue.dma_start(plane[32 * q : 32 * q + 4, :].bitcast(I32), scales[0, 4 * q : 4 * q + 4, :].bitcast(I32))


def tile_list_triple_looked_skip_scattered_kernel(
    tc, xt_words, xt_scales, w_words, w_scales, wb_words, wb_scales, sx_words, sx_scales, ws_words, ws_scales,
    offs, offs2, offs3, offs4, offs5, offs6, out,
):
    nc = tc.nc
    with ExitStack() as ctx:
        lists = ctx.enter_context(tc.tile_pool(name="lists", bufs=1))
        sb = ctx.enter_context(tc.tile_pool(name="sb", bufs=1))
        psum = ctx.enter_context(tc.psum_pool(name="psum", bufs=1))

        def load_list(src, name):
            tile = lists.tile(list(src.shape), U16, name=name)
            nc.sync.dma_start(tile[:], src)
            return tile

        xt_w = sb.tile([P, T], U16, name="xt_w", align_bytes=64)
        xt_s = sb.tile([P, T], U8, name="xt_s", align_bytes=64)
        w_raw = sb.tile([P, R], U32, name="w_raw", align_bytes=64)
        w_raw_s = sb.tile([P, R], U8, name="w_raw_s", align_bytes=64)
        w_w = sb.tile([P, R], U32, name="w_w", align_bytes=64)
        w_s = sb.tile([P, R], U8, name="w_s", align_bytes=64)
        wb_w = sb.tile([P, 2 * N], U8, name="wb_w", align_bytes=64)
        ws_w = sb.tile([P, N], U32, name="ws_w", align_bytes=64)
        sx_w = sb.tile([P, O], U32, name="sx_w", align_bytes=64)
        late_s = sb.tile([P, N + N + O], U8, name="late_s", align_bytes=64)
        wb_s, ws_s, sx_s = late_s[:, 0:N], late_s[:, N : 2 * N], late_s[:, 2 * N : 2 * N + O]
        pages = [sb.tile([P, E], F32, name=f"page{h}") for h in range(2)]

        nc.vector.memset(xt_s[:].bitcast(I32), 0)
        nc.gpsimd.memset(w_raw_s[:].bitcast(I32), 0)
        nc.gpsimd.memset(late_s[:].bitcast(I32), 0)

        nc.sync.dma_start(xt_w[:].bitcast(I32), xt_words[0].bitcast(I32))
        list_a = load_list(offs, "list_a")
        list_b = load_list(offs2, "list_b")
        load_scale_rows(nc.sync, xt_s, xt_scales)
        nc.sync.dma_start(w_raw[:].bitcast(I32), w_words[0].rearrange("p n t -> p (n t)").bitcast(I32))
        load_scale_rows(nc.sync, w_raw_s, w_scales)
        list_g = load_list(offs3, "list_g")
        pick_a = load_list(offs4, "pick_a")
        pick_c = load_list(offs5, "pick_c")
        nc.sync.dma_start(ws_w[:].bitcast(I32), ws_words[0].rearrange("p n t -> p (n t)").bitcast(I32))
        nc.sync.dma_start(sx_w[:].bitcast(I32), sx_words[0].rearrange("p n t -> p (n t)").bitcast(I32))
        nc.sync.dma_start(wb_w[:].bitcast(I32), wb_words[0].bitcast(I32))
        load_scale_rows(nc.sync, ws_s, ws_scales)
        load_scale_rows(nc.sync, sx_s, sx_scales)
        load_scale_rows(nc.sync, wb_s, wb_scales)
        places = load_list(offs6, "places")

        for page in pages:
            nc.vector.memset(page[:], 0.0)

        nc.scalar.copy(
            w_w[:].rearrange("p (t c i) -> p c t i", t=PACK, i=4),
            w_raw[:].rearrange("p (c i t) -> p c t i", t=PACK, i=4),
        )

        def gather_tokens(token_list, name):
            words = sb.tile([P, J], U16, name=name + "_w", align_bytes=64)
            scales = sb.tile([P, J], U8, name=name + "_s", align_bytes=64)
            nc.vector.tensor_copy(words[:], xt_w[:].indirect(token_list[:]))
            nc.vector.tensor_copy(scales[:], xt_s[:].indirect(token_list[:]))
            return words, scales

        def first_matrix(dst, t, tokens):
            words, scales = tokens
            cols = slice(t * P, (t + 1) * P)
            nc.tensor.matmul_mx(
                out=dst, lhsT=w_w[:, cols].bitcast(E4M3X4), lhsT_scale=w_s[:, cols],
                rhs=words[:].bitcast(E2M1X4), rhs_scale=scales[:], start=True, stop=True,
            )

        tokens_a = gather_tokens(list_a, "tok_a")
        tokens_b = gather_tokens(list_b, "tok_b")
        nc.vector.tensor_copy(
            w_s[:].rearrange("p (t c i) -> p c t i", t=PACK, i=16),
            w_raw_s[:].rearrange("p (c i t) -> p c t i", t=PACK, i=16),
        )
        tokens_g = gather_tokens(list_g, "tok_g")

        a_picked = sb.tile([P, PACK, O], F32, name="a_picked")
        diff = sb.tile([P, PACK, O], F32, name="diff")
        c1 = [sb.tile([P, J], F32, name=f"c1_{t}") for t in range(PACK)]

        def product(tokens, slots, name, bank):
            acc = psum.tile([P, len(slots), J], F32, name=name, tag=f"bank{bank}")
            for i, t in enumerate(slots):
                first_matrix(acc[:, i, :], t, tokens)
            return acc

        def to_sbuf(acc, name, tag):
            held = sb.tile(list(acc.shape), F32, name=name, tag=tag, align_bytes=64)
            nc.scalar.copy(held[:], acc[:])
            return held

        def pick_from_a(a_sb, slots):
            for i, t in enumerate(slots):
                nc.scalar.activation(a_picked[:, t, :], a_sb[:, i, :].indirect(pick_a[:]), ACT.Copy)

        def subtract(t):
            nc.vector.tensor_tensor(diff[:, t, :], c1[t][:].indirect(pick_c[:]), a_picked[:, t, :], ALU.subtract)

        pick_from_a(to_sbuf(product(tokens_a, [0], "a0", 0), "a0_sb", "a0_sb"), [0])
        bg0 = psum.tile([P, 2, J], F32, name="bg0", tag="bank2")
        first_matrix(bg0[:, 0, :], 0, tokens_b)
        pick_from_a(to_sbuf(product(tokens_a, [1], "a1", 1), "a1_sb", "a1_sb"), [1])
        b1_sb = to_sbuf(product(tokens_b, [1], "b1", 3), "b1_sb", "b1_sb")
        first_matrix(bg0[:, 1, :], 0, tokens_g)
        nc.vector.tensor_reduce(c1[0][:], bg0[:].rearrange("p s j -> p j s"), mybir.AxisListType.X, ALU.max)
        subtract(0)
        g1 = product(tokens_g, [1], "g1", 4)
        nc.vector.tensor_tensor(c1[1][:], g1[:, 0, :], b1_sb[:, 0, :], ALU.max)
        subtract(1)
        b23_sb = to_sbuf(product(tokens_b, [2, 3], "b23", 5), "b23_sb", "b23_sb")
        pick_from_a(to_sbuf(product(tokens_a, [2, 3], "a23", 6), "a23_sb", "a23_then_hid"), [2, 3])
        for t, bank in ((2, 7), (3, 0)):
            g_t = product(tokens_g, [t], f"g{t}", bank)
            nc.vector.tensor_tensor(c1[t][:], g_t[:, 0, :], b23_sb[:, t - 2, :], ALU.max)
        subtract(2)
        subtract(3)

        p_ps = [psum.tile([P, O], F32, name=f"p_ps{h}", tag=f"bank{1 + 2 * h}") for h in range(2)]
        for h in range(2):
            cols = slice(h * P, (h + 1) * P)
            nc.tensor.matmul_mx(
                out=p_ps[h][:], lhsT=ws_w[:, cols].bitcast(E4M3X4), lhsT_scale=ws_s[:, cols],
                rhs=sx_w[:].bitcast(E4M3X4), rhs_scale=sx_s, start=True, stop=False,
            )

        hid = sb.tile([P, O, PACK], BF16, name="hid", tag="a23_then_hid", align_bytes=64)
        by_place = diff[:].rearrange("p t o -> p o t")
        nc.scalar.activation(hid[:, :, 0:2], by_place[:, :, 0:2], ACT.Abs)
        nc.scalar.activation(hid[:, :O_SCALAR, 2:4], by_place[:, :O_SCALAR, 2:4], ACT.Abs)
        late = by_place[:, O_SCALAR:, 2:4]
        nc.vector.scalar_tensor_tensor(hid[:, O_SCALAR:, 2:4], late, -1.0, late, ALU.mult, ALU.max)
        hid_w = sb.tile([P, O], U32, name="hid_w", align_bytes=64)
        hid_s = sb.tile([P, O], U8, name="hid_s", align_bytes=64)
        nc.vector.quantize_mx(out=hid_w[:].bitcast(E5M2X4), scales=hid_s[:], in_=hid[:].rearrange("p o t -> p (o t)"))

        for h in range(2):
            nc.tensor.matmul_mx(
                out=p_ps[h][:], lhsT=wb_w[:, 2 * h * P : 2 * (h + 1) * P].bitcast(E2M1X4),
                lhsT_scale=wb_s[:, h * P : (h + 1) * P],
                rhs=hid_w[:].bitcast(E5M2X4), rhs_scale=hid_s[:], start=False, stop=True,
            )
        p_sb = [sb.tile([P, O], F32, name=f"p_sb{h}") for h in range(2)]
        nc.vector.tensor_copy(p_sb[0][:], p_ps[0][:])
        nc.vector.tensor_copy(pages[0][:].indirect(places[:]), p_sb[0][:])
        nc.sync.dma_start(out[0:P, :], pages[0][:])
        nc.scalar.copy(p_sb[1][:], p_ps[1][:])
        nc.scalar.activation(pages[1][:].indirect(places[:]), p_sb[1][:], ACT.Copy)
        nc.scalar.dma_start(out[P : 2 * P, :], pages[1][:])
